import numpy as np
import ml_dtypes


def mxq(x, axis, fmt="e4m3"):
    dtype, down = {"e4m3": (ml_dtypes.float8_e4m3fn, 7), "e5m2": (ml_dtypes.float8_e5m2, 14)}[fmt]
    v = np.moveaxis(np.asarray(x, np.float32).astype(ml_dtypes.bfloat16).astype(np.float64), axis, -1)
    blocks = v.reshape(v.shape[:-1] + (-1, 32))
    amax = np.abs(blocks).max(-1, keepdims=True)
    byte = np.maximum(np.where(amax > 0, np.frexp(amax)[1] - 1 + 127, 0) - down, 1)
    scale = np.exp2(byte - 127.0)
    codes = (blocks / scale).astype(np.float32).astype(dtype).astype(np.float64)
    return np.moveaxis((codes * scale).reshape(v.shape), -1, axis)


WIDE = False


def mx_kscale(k):
    if not WIDE:
        return np.ones(k)
    levels = np.array([10, -10, 5, -5, 0])
    if k % 512:
        return np.exp2(np.random.permutation(np.resize(levels, k // 32))).repeat(32)
    a = np.empty((k // 512, 16))
    for p in range(k // 512):
        a[p, :8] = np.random.permutation(np.resize(levels, 8))
        for g in range(8):
            far = levels[np.abs(levels - a[p, g]) >= 10]
            a[p, g + 8] = far[np.random.randint(len(far))]
    return np.exp2(a.ravel()).repeat(32)


def f64(x):
    return np.asarray(x).astype(np.float64)


def striped(idx):
    return np.tile(idx.reshape(-1, 16).T, (8, 1)).astype(np.uint16)


def unstriped(offs):
    return offs[:16].T.reshape(-1).astype(np.int64)


def striped8(idx):
    return np.concatenate([v.reshape(-1, 16).T for v in idx]).astype(np.uint16)


def unstriped8(offs):
    return np.stack([offs[16 * g:16 * g + 16].T.reshape(-1) for g in range(8)]).astype(np.int64)


E2M1 = np.array([0.0, 0.5, 1.0, 1.5, 2.0, 3.0, 4.0, 6.0, -0.0, -0.5, -1.0, -1.5, -2.0, -3.0, -4.0, -6.0])


def pack_weight(w, fmt):
    k, n = w.shape
    w = f64(np.asarray(w, np.float32).astype(ml_dtypes.bfloat16)).reshape(k // 32, 32, n)
    amax = np.abs(w).max(1)
    if fmt == "e4m3":
        byte = np.frexp(amax)[1] - 1 + 127 - 7
    else:
        mant, ex = np.frexp(amax / 6.0)
        byte = np.where(mant > 0.5, ex, ex - 1) + 127
    byte = np.clip(np.where(amax > 0, byte, 1), 1, 254)
    scaled = (w * np.exp2(127.0 - byte)[:, None, :]).reshape(k, n).astype(np.float32)
    by_word = np.ascontiguousarray(scaled.reshape(k // 512, 128, 4, n).transpose(0, 1, 3, 2))
    if fmt == "e4m3":
        words = by_word.astype(ml_dtypes.float8_e4m3fn).view(np.uint8)
    else:
        c = by_word.astype(ml_dtypes.float4_e2m1fn).view(np.uint8) & 0xF
        words = (c[..., 0::2] | (c[..., 1::2] << 4)).reshape(k // 512, 128, 2 * n)
    return np.ascontiguousarray(words), np.ascontiguousarray(byte.astype(np.uint8).reshape(k // 512, 16, n))


def unpack_weight(words, scales, fmt):
    g, _, n = scales.shape
    words = np.ascontiguousarray(words).reshape(g, 128, n, -1)
    if fmt == "e4m3":
        vals = words.view(ml_dtypes.float8_e4m3fn).astype(np.float64)
    else:
        nib = np.empty((g, 128, n, 4), np.uint8)
        nib[..., 0::2] = words & 0xF
        nib[..., 1::2] = words >> 4
        vals = E2M1[nib]
    vals = vals * np.repeat(np.exp2(scales.astype(np.float64) - 127.0), 8, axis=1)[..., None]
    return vals.transpose(0, 1, 3, 2).reshape(g * 512, n)


def pack_table(v):
    words, scales = pack_weight(v, "e4m3")
    return np.concatenate([words.reshape(words.shape[0], -1), scales.reshape(scales.shape[0], -1)], axis=1)


def unpack_table(tab):
    g, t = tab.shape[0], tab.shape[1] // 528
    return unpack_weight(tab[:, :512 * t].reshape(g, 128, t, 4), tab[:, 512 * t:].reshape(g, 16, t), "e4m3")


def silu(v):
    return v / (1.0 + np.exp(-np.maximum(v, -700.0)))


K, L, M, T, S = 512, 1536, 128, 2048, 512


def setup_inputs():
    n = np.random.standard_normal
    s1 = mx_kscale(K)[:, None]
    s2 = mx_kscale(L)[:, None]
    p_w4 = pack_weight(n((K, M)) / np.sqrt(K) / s1, "e2m1")
    return {
        "xT": (n((K, T)) * s1).astype(np.float32),
        "w4_words": p_w4[0],
        "w4_scales": p_w4[1],
        "tab": pack_table(n((L, T)) * s2),
        "u": (n((L, M)) / np.sqrt(L) / s2).astype(np.float32),
        "wgt": np.repeat(np.random.uniform(0.5, 2.0, (8, S)), 16, axis=0).astype(np.float32),
        "b": (0.3 * n(128)).astype(np.float32),
        "offs": striped(np.random.permutation(T)[:S]),
        "offs2": striped8(np.stack([np.random.permutation(T)[:S] for _ in range(8)])),
    }


def reference(xT, w4_words, w4_scales, tab, u, wgt, b, offs, offs2):
    idx2 = unstriped8(offs2)
    group = np.arange(K) % 512 // 64
    xg = f64(wgt)[np.arange(K) // 4 % 128] * f64(xT)[np.arange(K)[:, None], idx2[group]]
    xT_ = mxq(xg, 0, "e4m3")
    w4_ = unpack_weight(w4_words, w4_scales, "e2m1")
    tab_ = unpack_table(tab)[:, unstriped(offs)]
    u_ = mxq(f64(u), 0, "e4m3")
    y = xT_.T @ w4_ + tab_.T @ u_
    return silu(y + f64(b)[None, :])

@@ -1,0 +1,138 @@
+from contextlib import ExitStack
+
+import concourse.mybir as mybir
+from concourse.masks import make_identity
+
+K, L, M, T, S = 512, 1536, 128, 2048, 512
+FLOPS = 2 * (K + L) * M * S
+
+F32 = mybir.dt.float32
+BF16 = mybir.dt.bfloat16
+I32 = mybir.dt.int32
+U32 = mybir.dt.uint32
+U16 = mybir.dt.uint16
+U8 = mybir.dt.uint8
+FP8X4 = mybir.dt.float8_e4m3fn_x4
+FP4X4 = mybir.dt.float4_e2m1fn_x4
+MULT = mybir.AluOpType.mult
+SILU = mybir.ActivationFunctionType.Silu
+
+P = 128
+PACK = 4
+PASSES = L // (P * PACK)
+QUADS = 4
+CHUNK = 128
+CHUNKS = S // CHUNK
+GROUP = 16
+
+
+def tile_list_htab_tm_silu_kernel(tc, xT, w4_words, w4_scales, tab, u, wgt, b, offs, offs2, out):
+    nc = tc.nc
+    tab32 = tab.bitcast(I32)
+    with ExitStack() as ctx:
+        lists = ctx.enter_context(tc.tile_pool(name="lists", bufs=1))
+        sb = ctx.enter_context(tc.tile_pool(name="sb", bufs=1))
+        ps = ctx.enter_context(tc.psum_pool(name="ps", bufs=1))
+
+        offs_t = lists.tile([P, S // GROUP], U16, name="offs_t")
+        offs2_t = lists.tile([P, S // GROUP], U16, name="offs2_t")
+
+        x_planes = [sb.tile([P, T], F32, name="x_plane%d" % i) for i in range(PACK)]
+        tab_words = [sb.tile([P, T], U32, name="tab_words%d" % a) for a in range(PASSES)]
+        tab_scales = sb.tile([P, T], U8, name="tab_scales")
+        wgt_t = sb.tile([P, S], F32, name="wgt_t")
+        u_raw = sb.tile([P, PASSES, PACK, M], F32, name="u_raw")
+        w4_t = sb.tile([P, 2 * M], U8, name="w4_t", align_bytes=64)
+        w4_s = sb.tile([P, M], U8, name="w4_s", align_bytes=64)
+        b_col = sb.tile([P, 1], F32, name="b_col")
+        ident = sb.tile([P, P], F32, name="ident")
+
+        nc.gpsimd.memset(tab_scales[:].bitcast(I32), 0)
+        scale_rows = tab32[:, P * T:].rearrange("a (q t) -> a q t", t=T // 4)
+        for q in range(QUADS):
+            nc.gpsimd.dma_start(
+                out=tab_scales[32 * q: 32 * q + 4 * PASSES, :].bitcast(I32),
+                in_=scale_rows[:, 4 * q: 4 * q + 4, :],
+            )
+        nc.gpsimd.memset(w4_s[:].bitcast(I32), 0)
+        for q in range(QUADS):
+            nc.gpsimd.dma_start(
+                out=w4_s[32 * q: 32 * q + 4, :].bitcast(I32),
+                in_=w4_scales[0, 4 * q: 4 * q + 4, :].bitcast(I32),
+            )
+        make_identity(nc, ident[:])
+
+        x_rows = xT.rearrange("(p i) t -> i p t", i=PACK)
+        nc.sync.dma_start(out=x_planes[0][:], in_=x_rows[0])
+        nc.sync.dma_start(offs2_t[:], offs2)
+        nc.sync.dma_start(out=wgt_t[:], in_=wgt)
+        for i in range(1, PACK):
+            nc.sync.dma_start(out=x_planes[i][:], in_=x_rows[i])
+        nc.sync.dma_start(offs_t[:], offs)
+        nc.sync.dma_start(
+            out=u_raw[:].rearrange("p a i n -> p a (i n)"),
+            in_=u.rearrange("(a p i) n -> p a (i n)", p=P, i=PACK),
+        )
+        for a in range(PASSES):
+            if a == 1:
+                nc.sync.dma_start(out=w4_t[:].bitcast(I32), in_=w4_words[0].bitcast(I32))
+                with nc.allow_non_contiguous_dma(reason="one bias value a partition"):
+                    nc.sync.dma_start(out=b_col[:], in_=b.rearrange("(p o) -> p o", o=1))
+            nc.sync.dma_start(
+                out=tab_words[a][:].bitcast(I32),
+                in_=tab32[a, 0: P * T].rearrange("(p t) -> p t", p=P),
+            )
+
+        xg = sb.tile([P, PACK, S], F32, name="xg")
+        for i in range(PACK):
+            nc.vector.tensor_tensor(xg[:, i, :], x_planes[i][:].indirect(offs2_t[:]), wgt_t[:], MULT)
+        got_scales = sb.tile([P, S], U8, name="got_scales", align_bytes=64)
+        nc.vector.tensor_copy(got_scales[:], tab_scales[:].indirect(offs_t[:]))
+        xg16 = sb.tile([P, S, PACK], BF16, name="xg16", align_bytes=64)
+        nc.vector.tensor_copy(
+            out=xg16[:].rearrange("p (c e) i -> p c i e", e=4),
+            in_=xg[:].rearrange("p i (c e) -> p c i e", e=4),
+        )
+        x_codes = sb.tile([P, S], U32, name="x_codes", align_bytes=64)
+        x_scales = sb.tile([P, S], U8, name="x_scales", align_bytes=64)
+        nc.vector.quantize_mx(out=x_codes[:].bitcast(FP8X4), scales=x_scales[:], in_=xg16[:].rearrange("p j i -> p (j i)"))
+
+        u16 = sb.tile([P, PASSES, M, PACK], BF16, name="u16", align_bytes=64)
+        nc.scalar.copy(out=u16[:], in_=u_raw[:].rearrange("p a i n -> p a n i"))
+        u_codes = sb.tile([P, PASSES * M], U32, name="u_codes", align_bytes=64)
+        u_scales = sb.tile([P, PASSES * M], U8, name="u_scales", align_bytes=64)
+        nc.vector.quantize_mx(out=u_codes[:].bitcast(FP8X4), scales=u_scales[:], in_=u16[:].rearrange("p a n i -> p (a n i)"))
+
+        acc = [ps.tile([P, CHUNK], F32, name="acc%d" % c) for c in range(CHUNKS)]
+        for c in range(CHUNKS):
+            cols = slice(c * CHUNK, (c + 1) * CHUNK)
+            nc.tensor.matmul_mx(
+                out=acc[c][:], lhsT=w4_t[:].bitcast(FP4X4), lhsT_scale=w4_s[:],
+                rhs=x_codes[:, cols].bitcast(FP8X4), rhs_scale=x_scales[:, cols], start=True, stop=False,
+            )
+
+        got_words = [sb.tile([P, S], U32, name="got_words%d" % a, align_bytes=64) for a in range(PASSES)]
+        for a in range(PASSES):
+            last = a == PASSES - 1
+            if not last:
+                nc.vector.tensor_copy(got_words[a][:], tab_words[a][:].indirect(offs_t[:]))
+            for c in range(CHUNKS):
+                cols = slice(c * CHUNK, (c + 1) * CHUNK)
+                if last:
+                    entries = offs_t[:, c * CHUNK // GROUP: (c + 1) * CHUNK // GROUP]
+                    nc.vector.tensor_copy(got_words[a][:, cols], tab_words[a][:].indirect(entries))
+                nc.tensor.matmul_mx(
+                    out=acc[c][:],
+                    lhsT=u_codes[:, a * M: (a + 1) * M].bitcast(FP8X4), lhsT_scale=u_scales[:, a * M: (a + 1) * M],
+                    rhs=got_words[a][:, cols].bitcast(FP8X4), rhs_scale=got_scales[4 * a: P, cols],
+                    start=False, stop=last,
+                )
+
+        for c in range(CHUNKS):
+            act = sb.tile([P, CHUNK], F32, name="act%d" % c)
+            nc.scalar.activation(out=act[:], in_=acc[c][:], func=SILU, bias=b_col[:])
+            turned = ps.tile([P, M], F32, name="turned%d" % c)
+            nc.tensor.transpose(turned[:], act[:], ident[:])
+            res = sb.tile([P, M], F32, name="res%d" % c)
+            nc.vector.tensor_copy(out=res[:], in_=turned[:])
+            nc.sync.dma_start(out=out[c * CHUNK: (c + 1) * CHUNK, :], in_=res[:])

@@ -15,6 +15,7 @@ U8 = mybir.dt.uint8
 FP8X4 = mybir.dt.float8_e4m3fn_x4
 FP4X4 = mybir.dt.float4_e2m1fn_x4
 MULT = mybir.AluOpType.mult
+ADD = mybir.AluOpType.add
 SILU = mybir.ActivationFunctionType.Silu
 
 P = 128
@@ -54,21 +55,23 @@ def tile_list_htab_tm_silu_kernel(tc, xT, w4_words, w4_scales, tab, u, wgt, b, o
                 out=tab_scales[32 * q: 32 * q + 4 * PASSES, :].bitcast(I32),
                 in_=scale_rows[:, 4 * q: 4 * q + 4, :],
             )
+        make_identity(nc, ident[:])
         nc.gpsimd.memset(w4_s[:].bitcast(I32), 0)
         for q in range(QUADS):
             nc.gpsimd.dma_start(
                 out=w4_s[32 * q: 32 * q + 4, :].bitcast(I32),
                 in_=w4_scales[0, 4 * q: 4 * q + 4, :].bitcast(I32),
             )
-        make_identity(nc, ident[:])
 
         x_rows = xT.rearrange("(p i) t -> i p t", i=PACK)
         nc.sync.dma_start(out=x_planes[0][:], in_=x_rows[0])
         nc.sync.dma_start(offs2_t[:], offs2)
         nc.sync.dma_start(out=wgt_t[:], in_=wgt)
+        nc.sync.dma_start(offs_t[:], offs)
+        with nc.allow_non_contiguous_dma(reason="one bias value a partition"):
+            nc.sync.dma_start(out=b_col[:], in_=b.rearrange("(p o) -> p o", o=1))
         for i in range(1, PACK):
             nc.sync.dma_start(out=x_planes[i][:], in_=x_rows[i])
-        nc.sync.dma_start(offs_t[:], offs)
         nc.sync.dma_start(
             out=u_raw[:].rearrange("p a i n -> p a (i n)"),
             in_=u.rearrange("(a p i) n -> p a (i n)", p=P, i=PACK),
@@ -76,22 +79,27 @@ def tile_list_htab_tm_silu_kernel(tc, xT, w4_words, w4_scales, tab, u, wgt, b, o
         for a in range(PASSES):
             if a == 1:
                 nc.sync.dma_start(out=w4_t[:].bitcast(I32), in_=w4_words[0].bitcast(I32))
-                with nc.allow_non_contiguous_dma(reason="one bias value a partition"):
-                    nc.sync.dma_start(out=b_col[:], in_=b.rearrange("(p o) -> p o", o=1))
             nc.sync.dma_start(
                 out=tab_words[a][:].bitcast(I32),
                 in_=tab32[a, 0: P * T].rearrange("(p t) -> p t", p=P),
             )
 
+        b_ps = ps.tile([P, M], F32, name="b_ps")
+        nc.tensor.transpose(b_ps[:], b_col[:].to_broadcast([P, P]), ident[:])
+        b_rows = sb.tile([P, M], F32, name="b_rows")
+        nc.scalar.copy(out=b_rows[:], in_=b_ps[:])
+
         xg = sb.tile([P, PACK, S], F32, name="xg")
+        got_scales = sb.tile([P, S], U8, name="got_scales", align_bytes=64)
         for i in range(PACK):
             nc.vector.tensor_tensor(xg[:, i, :], x_planes[i][:].indirect(offs2_t[:]), wgt_t[:], MULT)
-        got_scales = sb.tile([P, S], U8, name="got_scales", align_bytes=64)
-        nc.vector.tensor_copy(got_scales[:], tab_scales[:].indirect(offs_t[:]))
+            if i == 1:
+                nc.vector.tensor_copy(got_scales[:], tab_scales[:].indirect(offs_t[:]))
         xg16 = sb.tile([P, S, PACK], BF16, name="xg16", align_bytes=64)
+        nc.scalar.copy(out=xg16[:, 0: S // 2, :], in_=xg[:, :, 0: S // 2].rearrange("p i j -> p j i"))
         nc.vector.tensor_copy(
-            out=xg16[:].rearrange("p (c e) i -> p c i e", e=4),
-            in_=xg[:].rearrange("p i (c e) -> p c i e", e=4),
+            out=xg16[:, S // 2: S, :].rearrange("p (c e) i -> p c i e", e=4),
+            in_=xg[:, :, S // 2: S].rearrange("p i (c e) -> p c i e", e=4),
         )
         x_codes = sb.tile([P, S], U32, name="x_codes", align_bytes=64)
         x_scales = sb.tile([P, S], U8, name="x_scales", align_bytes=64)
@@ -103,12 +111,12 @@ def tile_list_htab_tm_silu_kernel(tc, xT, w4_words, w4_scales, tab, u, wgt, b, o
         u_scales = sb.tile([P, PASSES * M], U8, name="u_scales", align_bytes=64)
         nc.vector.quantize_mx(out=u_codes[:].bitcast(FP8X4), scales=u_scales[:], in_=u16[:].rearrange("p a n i -> p (a n i)"))
 
-        acc = [ps.tile([P, CHUNK], F32, name="acc%d" % c) for c in range(CHUNKS)]
+        acc = [ps.tile([CHUNK, M], F32, name="acc%d" % c) for c in range(CHUNKS)]
         for c in range(CHUNKS):
             cols = slice(c * CHUNK, (c + 1) * CHUNK)
             nc.tensor.matmul_mx(
-                out=acc[c][:], lhsT=w4_t[:].bitcast(FP4X4), lhsT_scale=w4_s[:],
-                rhs=x_codes[:, cols].bitcast(FP8X4), rhs_scale=x_scales[:, cols], start=True, stop=False,
+                out=acc[c][:], lhsT=x_codes[:, cols].bitcast(FP8X4), lhsT_scale=x_scales[:, cols],
+                rhs=w4_t[:].bitcast(FP4X4), rhs_scale=w4_s[:], start=True, stop=False,
             )
 
         got_words = [sb.tile([P, S], U32, name="got_words%d" % a, align_bytes=64) for a in range(PASSES)]
@@ -123,16 +131,14 @@ def tile_list_htab_tm_silu_kernel(tc, xT, w4_words, w4_scales, tab, u, wgt, b, o
                     nc.vector.tensor_copy(got_words[a][:, cols], tab_words[a][:].indirect(entries))
                 nc.tensor.matmul_mx(
                     out=acc[c][:],
-                    lhsT=u_codes[:, a * M: (a + 1) * M].bitcast(FP8X4), lhsT_scale=u_scales[:, a * M: (a + 1) * M],
-                    rhs=got_words[a][:, cols].bitcast(FP8X4), rhs_scale=got_scales[4 * a: P, cols],
+                    lhsT=got_words[a][:, cols].bitcast(FP8X4), lhsT_scale=got_scales[4 * a: P, cols],
+                    rhs=u_codes[:, a * M: (a + 1) * M].bitcast(FP8X4), rhs_scale=u_scales[:, a * M: (a + 1) * M],
                     start=False, stop=last,
                 )
 
         for c in range(CHUNKS):
-            act = sb.tile([P, CHUNK], F32, name="act%d" % c)
-            nc.scalar.activation(out=act[:], in_=acc[c][:], func=SILU, bias=b_col[:])
-            turned = ps.tile([P, M], F32, name="turned%d" % c)
-            nc.tensor.transpose(turned[:], act[:], ident[:])
+            biased = sb.tile([P, M], F32, name="biased%d" % c)
+            nc.vector.tensor_tensor(biased[:], acc[c][:], b_rows[:], ADD)
             res = sb.tile([P, M], F32, name="res%d" % c)
-            nc.vector.tensor_copy(out=res[:], in_=turned[:])
+            nc.scalar.activation(out=res[:], in_=biased[:], func=SILU)
             nc.sync.dma_start(out=out[c * CHUNK: (c + 1) * CHUNK, :], in_=res[:])

@@ -49,40 +49,61 @@ def tile_list_htab_tm_silu_kernel(tc, xT, w4_words, w4_scales, tab, u, wgt, b, o
         ident = sb.tile([P, P], F32, name="ident")
 
         nc.gpsimd.memset(tab_scales[:].bitcast(I32), 0)
-        scale_rows = tab32[:, P * T:].rearrange("a (q t) -> a q t", t=T // 4)
-        for q in range(QUADS):
-            nc.gpsimd.dma_start(
-                out=tab_scales[32 * q: 32 * q + 4 * PASSES, :].bitcast(I32),
-                in_=scale_rows[:, 4 * q: 4 * q + 4, :],
-            )
         make_identity(nc, ident[:])
         nc.gpsimd.memset(w4_s[:].bitcast(I32), 0)
-        for q in range(QUADS):
-            nc.gpsimd.dma_start(
-                out=w4_s[32 * q: 32 * q + 4, :].bitcast(I32),
-                in_=w4_scales[0, 4 * q: 4 * q + 4, :].bitcast(I32),
-            )
 
         x_rows = xT.rearrange("(p i) t -> i p t", i=PACK)
-        nc.sync.dma_start(out=x_planes[0][:], in_=x_rows[0])
-        nc.sync.dma_start(offs2_t[:], offs2)
-        nc.sync.dma_start(out=wgt_t[:], in_=wgt)
-        nc.sync.dma_start(offs_t[:], offs)
-        with nc.allow_non_contiguous_dma(reason="one bias value a partition"):
-            nc.sync.dma_start(out=b_col[:], in_=b.rearrange("(p o) -> p o", o=1))
-        for i in range(1, PACK):
+        scale_rows = tab32[:, P * T:].rearrange("a (q t) -> a q t", t=T // 4)
+
+        def load_x(i):
             nc.sync.dma_start(out=x_planes[i][:], in_=x_rows[i])
-        nc.sync.dma_start(
-            out=u_raw[:].rearrange("p a i n -> p a (i n)"),
-            in_=u.rearrange("(a p i) n -> p a (i n)", p=P, i=PACK),
-        )
-        for a in range(PASSES):
-            if a == 1:
-                nc.sync.dma_start(out=w4_t[:].bitcast(I32), in_=w4_words[0].bitcast(I32))
+
+        def load_words(a):
             nc.sync.dma_start(
                 out=tab_words[a][:].bitcast(I32),
                 in_=tab32[a, 0: P * T].rearrange("(p t) -> p t", p=P),
             )
+
+        wgt_quarter = sb.tile([P, P], F32, name="wgt_quarter")
+        nc.sync.dma_start(out=wgt_quarter[:], in_=wgt.rearrange("(r f) (c e) -> f r c e", f=4, c=4)[0])
+        load_x(0)
+        nc.sync.dma_start(offs2_t[:], offs2)
+        load_x(1)
+        for q in range(QUADS):
+            nc.sync.dma_start(
+                out=tab_scales[32 * q: 32 * q + 4 * PASSES, :].bitcast(I32),
+                in_=scale_rows[:, 4 * q: 4 * q + 4, :],
+            )
+        load_x(2)
+        nc.sync.dma_start(offs_t[:], offs)
+        load_x(3)
+        with nc.allow_non_contiguous_dma(reason="one bias value a partition"):
+            nc.sync.dma_start(out=b_col[:], in_=b.rearrange("(p o) -> p o", o=1))
+        nc.sync.dma_start(
+            out=u_raw[:].rearrange("p a i n -> p a (i n)"),
+            in_=u.rearrange("(a p i) n -> p a (i n)", p=P, i=PACK),
+        )
+        for q in range(QUADS):
+            nc.sync.dma_start(
+                out=w4_s[32 * q: 32 * q + 4, :].bitcast(I32),
+                in_=w4_scales[0, 4 * q: 4 * q + 4, :].bitcast(I32),
+            )
+        load_words(0)
+        nc.sync.dma_start(out=w4_t[:].bitcast(I32), in_=w4_words[0].bitcast(I32))
+        load_words(1)
+        load_words(2)
+
+        quarter_ps = ps.tile([P, P], F32, name="quarter_ps")
+        nc.tensor.transpose(quarter_ps[:], wgt_quarter[:], ident[:])
+        wgt_cols = sb.tile([P, 4, P], F32, name="wgt_cols")
+        nc.scalar.copy(
+            out=wgt_cols[:].rearrange("e c (r f) -> e c r f", f=4),
+            in_=quarter_ps[:].rearrange("e (r c) -> e c r", c=4).unsqueeze(3).to_broadcast([P, 4, P // 4, 4]),
+        )
+        wgt_ps = ps.tile([P, 4, P], F32, name="wgt_ps")
+        for c in range(4):
+            nc.tensor.transpose(wgt_ps[:, c, :], wgt_cols[:, c, :], ident[:])
+        nc.scalar.copy(out=wgt_t[:], in_=wgt_ps[:].rearrange("p c e -> p (c e)"))
 
         b_ps = ps.tile([P, M], F32, name="b_ps")
         nc.tensor.transpose(b_ps[:], b_col[:].to_broadcast([P, P]), ident[:])
@@ -93,7 +114,7 @@ def tile_list_htab_tm_silu_kernel(tc, xT, w4_words, w4_scales, tab, u, wgt, b, o
         got_scales = sb.tile([P, S], U8, name="got_scales", align_bytes=64)
         for i in range(PACK):
             nc.vector.tensor_tensor(xg[:, i, :], x_planes[i][:].indirect(offs2_t[:]), wgt_t[:], MULT)
-            if i == 1:
+            if i == 2:
                 nc.vector.tensor_copy(got_scales[:], tab_scales[:].indirect(offs_t[:]))
         xg16 = sb.tile([P, S, PACK], BF16, name="xg16", align_bytes=64)
         nc.scalar.copy(out=xg16[:, 0: S // 2, :], in_=xg[:, :, 0: S // 2].rearrange("p i j -> p j i"))
@@ -141,4 +162,5 @@ def tile_list_htab_tm_silu_kernel(tc, xT, w4_words, w4_scales, tab, u, wgt, b, o
             nc.vector.tensor_tensor(biased[:], acc[c][:], b_rows[:], ADD)
             res = sb.tile([P, M], F32, name="res%d" % c)
             nc.scalar.activation(out=res[:], in_=biased[:], func=SILU)
-            nc.sync.dma_start(out=out[c * CHUNK: (c + 1) * CHUNK, :], in_=res[:])
+            queue = nc.scalar if c == CHUNKS - 1 else nc.sync
+            queue.dma_start(out=out[c * CHUNK: (c + 1) * CHUNK, :], in_=res[:])

from contextlib import ExitStack

import concourse.mybir as mybir
from concourse.masks import make_identity

K, L, M, T, S = 512, 1536, 128, 2048, 512
FLOPS = 2 * (K + L) * M * S

F32 = mybir.dt.float32
BF16 = mybir.dt.bfloat16
I32 = mybir.dt.int32
U32 = mybir.dt.uint32
U16 = mybir.dt.uint16
U8 = mybir.dt.uint8
FP8X4 = mybir.dt.float8_e4m3fn_x4
FP4X4 = mybir.dt.float4_e2m1fn_x4
MULT = mybir.AluOpType.mult
ADD = mybir.AluOpType.add
SILU = mybir.ActivationFunctionType.Silu

P = 128
PACK = 4
PASSES = L // (P * PACK)
QUADS = 4
CHUNK = 128
CHUNKS = S // CHUNK
GROUP = 16


def tile_list_htab_tm_silu_kernel(tc, xT, w4_words, w4_scales, tab, u, wgt, b, offs, offs2, out):
    nc = tc.nc
    tab32 = tab.bitcast(I32)
    with ExitStack() as ctx:
        lists = ctx.enter_context(tc.tile_pool(name="lists", bufs=1))
        sb = ctx.enter_context(tc.tile_pool(name="sb", bufs=1))
        ps = ctx.enter_context(tc.psum_pool(name="ps", bufs=1))

        offs_t = lists.tile([P, S // GROUP], U16, name="offs_t")
        offs2_t = lists.tile([P, S // GROUP], U16, name="offs2_t")

        x_planes = [sb.tile([P, T], F32, name="x_plane%d" % i) for i in range(PACK)]
        tab_words = [sb.tile([P, T], U32, name="tab_words%d" % a) for a in range(PASSES)]
        tab_scales = sb.tile([P, T], U8, name="tab_scales")
        wgt_t = sb.tile([P, S], F32, name="wgt_t")
        u_raw = sb.tile([P, PASSES, PACK, M], F32, name="u_raw")
        w4_t = sb.tile([P, 2 * M], U8, name="w4_t", align_bytes=64)
        w4_s = sb.tile([P, M], U8, name="w4_s", align_bytes=64)
        b_col = sb.tile([P, 1], F32, name="b_col")
        ident = sb.tile([P, P], F32, name="ident")

        nc.gpsimd.memset(tab_scales[:].bitcast(I32), 0)
        make_identity(nc, ident[:])
        nc.gpsimd.memset(w4_s[:].bitcast(I32), 0)

        x_rows = xT.rearrange("(p i) t -> i p t", i=PACK)
        scale_rows = tab32[:, P * T:].rearrange("a (q t) -> a q t", t=T // 4)

        def load_x(i):
            nc.sync.dma_start(out=x_planes[i][:], in_=x_rows[i])

        def load_words(a):
            nc.sync.dma_start(
                out=tab_words[a][:].bitcast(I32),
                in_=tab32[a, 0: P * T].rearrange("(p t) -> p t", p=P),
            )

        wgt_quarter = sb.tile([P, P], F32, name="wgt_quarter")
        nc.sync.dma_start(out=wgt_quarter[:], in_=wgt.rearrange("(r f) (c e) -> f r c e", f=4, c=4)[0])
        load_x(0)
        nc.sync.dma_start(offs2_t[:], offs2)
        load_x(1)
        for q in range(QUADS):
            nc.sync.dma_start(
                out=tab_scales[32 * q: 32 * q + 4 * PASSES, :].bitcast(I32),
                in_=scale_rows[:, 4 * q: 4 * q + 4, :],
            )
        load_x(2)
        nc.sync.dma_start(offs_t[:], offs)
        load_x(3)
        with nc.allow_non_contiguous_dma(reason="one bias value a partition"):
            nc.sync.dma_start(out=b_col[:], in_=b.rearrange("(p o) -> p o", o=1))
        nc.sync.dma_start(
            out=u_raw[:].rearrange("p a i n -> p a (i n)"),
            in_=u.rearrange("(a p i) n -> p a (i n)", p=P, i=PACK),
        )
        for q in range(QUADS):
            nc.sync.dma_start(
                out=w4_s[32 * q: 32 * q + 4, :].bitcast(I32),
                in_=w4_scales[0, 4 * q: 4 * q + 4, :].bitcast(I32),
            )
        load_words(0)
        nc.sync.dma_start(out=w4_t[:].bitcast(I32), in_=w4_words[0].bitcast(I32))
        load_words(1)
        load_words(2)

        quarter_ps = ps.tile([P, P], F32, name="quarter_ps")
        nc.tensor.transpose(quarter_ps[:], wgt_quarter[:], ident[:])
        wgt_cols = sb.tile([P, 4, P], F32, name="wgt_cols")
        nc.scalar.copy(
            out=wgt_cols[:].rearrange("e c (r f) -> e c r f", f=4),
            in_=quarter_ps[:].rearrange("e (r c) -> e c r", c=4).unsqueeze(3).to_broadcast([P, 4, P // 4, 4]),
        )
        wgt_ps = ps.tile([P, 4, P], F32, name="wgt_ps")
        for c in range(4):
            nc.tensor.transpose(wgt_ps[:, c, :], wgt_cols[:, c, :], ident[:])
        nc.scalar.copy(out=wgt_t[:], in_=wgt_ps[:].rearrange("p c e -> p (c e)"))

        b_ps = ps.tile([P, M], F32, name="b_ps")
        nc.tensor.transpose(b_ps[:], b_col[:].to_broadcast([P, P]), ident[:])
        b_rows = sb.tile([P, M], F32, name="b_rows")
        nc.scalar.copy(out=b_rows[:], in_=b_ps[:])

        xg = sb.tile([P, PACK, S], F32, name="xg")
        got_scales = sb.tile([P, S], U8, name="got_scales", align_bytes=64)
        for i in range(PACK):
            nc.vector.tensor_tensor(xg[:, i, :], x_planes[i][:].indirect(offs2_t[:]), wgt_t[:], MULT)
            if i == 2:
                nc.vector.tensor_copy(got_scales[:], tab_scales[:].indirect(offs_t[:]))
        xg16 = sb.tile([P, S, PACK], BF16, name="xg16", align_bytes=64)
        nc.scalar.copy(out=xg16[:, 0: S // 2, :], in_=xg[:, :, 0: S // 2].rearrange("p i j -> p j i"))
        nc.vector.tensor_copy(
            out=xg16[:, S // 2: S, :].rearrange("p (c e) i -> p c i e", e=4),
            in_=xg[:, :, S // 2: S].rearrange("p i (c e) -> p c i e", e=4),
        )
        x_codes = sb.tile([P, S], U32, name="x_codes", align_bytes=64)
        x_scales = sb.tile([P, S], U8, name="x_scales", align_bytes=64)
        nc.vector.quantize_mx(out=x_codes[:].bitcast(FP8X4), scales=x_scales[:], in_=xg16[:].rearrange("p j i -> p (j i)"))

        u16 = sb.tile([P, PASSES, M, PACK], BF16, name="u16", align_bytes=64)
        nc.scalar.copy(out=u16[:], in_=u_raw[:].rearrange("p a i n -> p a n i"))
        u_codes = sb.tile([P, PASSES * M], U32, name="u_codes", align_bytes=64)
        u_scales = sb.tile([P, PASSES * M], U8, name="u_scales", align_bytes=64)
        nc.vector.quantize_mx(out=u_codes[:].bitcast(FP8X4), scales=u_scales[:], in_=u16[:].rearrange("p a n i -> p (a n i)"))

        acc = [ps.tile([CHUNK, M], F32, name="acc%d" % c) for c in range(CHUNKS)]
        for c in range(CHUNKS):
            cols = slice(c * CHUNK, (c + 1) * CHUNK)
            nc.tensor.matmul_mx(
                out=acc[c][:], lhsT=x_codes[:, cols].bitcast(FP8X4), lhsT_scale=x_scales[:, cols],
                rhs=w4_t[:].bitcast(FP4X4), rhs_scale=w4_s[:], start=True, stop=False,
            )

        got_words = [sb.tile([P, S], U32, name="got_words%d" % a, align_bytes=64) for a in range(PASSES)]
        for a in range(PASSES):
            last = a == PASSES - 1
            if not last:
                nc.vector.tensor_copy(got_words[a][:], tab_words[a][:].indirect(offs_t[:]))
            for c in range(CHUNKS):
                cols = slice(c * CHUNK, (c + 1) * CHUNK)
                if last:
                    entries = offs_t[:, c * CHUNK // GROUP: (c + 1) * CHUNK // GROUP]
                    nc.vector.tensor_copy(got_words[a][:, cols], tab_words[a][:].indirect(entries))
                nc.tensor.matmul_mx(
                    out=acc[c][:],
                    lhsT=got_words[a][:, cols].bitcast(FP8X4), lhsT_scale=got_scales[4 * a: P, cols],
                    rhs=u_codes[:, a * M: (a + 1) * M].bitcast(FP8X4), rhs_scale=u_scales[:, a * M: (a + 1) * M],
                    start=False, stop=last,
                )

        for c in range(CHUNKS):
            biased = sb.tile([P, M], F32, name="biased%d" % c)
            nc.vector.tensor_tensor(biased[:], acc[c][:], b_rows[:], ADD)
            res = sb.tile([P, M], F32, name="res%d" % c)
            nc.scalar.activation(out=res[:], in_=biased[:], func=SILU)
            queue = nc.scalar if c == CHUNKS - 1 else nc.sync
            queue.dma_start(out=out[c * CHUNK: (c + 1) * CHUNK, :], in_=res[:])
